import numpy as np
import ml_dtypes


def mxq(x, axis, fmt="e4m3"):
    dtype, down = {"e4m3": (ml_dtypes.float8_e4m3fn, 7), "e5m2": (ml_dtypes.float8_e5m2, 14)}[fmt]
    v = np.moveaxis(np.asarray(x, np.float32).astype(ml_dtypes.bfloat16).astype(np.float64), axis, -1)
    blocks = v.reshape(v.shape[:-1] + (-1, 32))
    amax = np.abs(blocks).max(-1, keepdims=True)
    byte = np.maximum(np.where(amax > 0, np.frexp(amax)[1] - 1 + 127, 0) - down, 1)
    scale = np.exp2(byte - 127.0)
    codes = (blocks / scale).astype(np.float32).astype(dtype).astype(np.float64)
    return np.moveaxis((codes * scale).reshape(v.shape), -1, axis)


WIDE = False


def mx_kscale(k):
    if not WIDE:
        return np.ones(k)
    levels = np.array([30, -30])
    if k % 512:
        return np.exp2(np.random.permutation(np.resize(levels, k // 32))).repeat(32)
    a = np.empty((k // 512, 16))
    for p in range(k // 512):
        a[p, :8] = np.random.permutation(np.resize(levels, 8))
        for g in range(8):
            far = levels[np.abs(levels - a[p, g]) >= 10]
            a[p, g + 8] = far[np.random.randint(len(far))]
    return np.exp2(a.ravel()).repeat(32)


def f64(x):
    return np.asarray(x).astype(np.float64)


def striped(idx):
    return np.tile(np.asarray(idx).reshape(-1, 16).T, (8, 1)).astype(np.uint16)


def unstriped(offs):
    return offs[:16].T.reshape(-1).astype(np.int64)


E2M1 = np.array([0.0, 0.5, 1.0, 1.5, 2.0, 3.0, 4.0, 6.0, -0.0, -0.5, -1.0, -1.5, -2.0, -3.0, -4.0, -6.0])


def pack_weight(w, fmt):
    k, n = w.shape
    w = f64(np.asarray(w, np.float32).astype(ml_dtypes.bfloat16)).reshape(k // 32, 32, n)
    amax = np.abs(w).max(1)
    if fmt in ("e4m3", "e5m2"):
        byte = np.frexp(amax)[1] - 1 + 127 - (7 if fmt == "e4m3" else 14)
    else:
        mant, ex = np.frexp(amax / 6.0)
        byte = np.where(mant > 0.5, ex, ex - 1) + 127
    byte = np.clip(np.where(amax > 0, byte, 1), 1, 254)
    scaled = (w * np.exp2(127.0 - byte)[:, None, :]).reshape(k, n).astype(np.float32)
    by_word = np.ascontiguousarray(scaled.reshape(k // 512, 128, 4, n).transpose(0, 1, 3, 2))
    if fmt in ("e4m3", "e5m2"):
        words = by_word.astype(ml_dtypes.float8_e4m3fn if fmt == "e4m3" else ml_dtypes.float8_e5m2).view(np.uint8)
    else:
        c = by_word.astype(ml_dtypes.float4_e2m1fn).view(np.uint8) & 0xF
        words = (c[..., 0::2] | (c[..., 1::2] << 4)).reshape(k // 512, 128, 2 * n)
    return np.ascontiguousarray(words), np.ascontiguousarray(byte.astype(np.uint8).reshape(k // 512, 16, n))


def unpack_weight(words, scales, fmt):
    g, _, n = scales.shape
    words = np.ascontiguousarray(words).reshape(g, 128, n, -1)
    if fmt in ("e4m3", "e5m2"):
        vals = words.view(ml_dtypes.float8_e4m3fn if fmt == "e4m3" else ml_dtypes.float8_e5m2).astype(np.float64)
    else:
        nib = np.empty((g, 128, n, 4), np.uint8)
        nib[..., 0::2] = words & 0xF
        nib[..., 1::2] = words >> 4
        vals = E2M1[nib]
    vals = vals * np.repeat(np.exp2(scales.astype(np.float64) - 127.0), 8, axis=1)[..., None]
    return vals.transpose(0, 1, 3, 2).reshape(g * 512, n)


def sgn(shape):
    return np.random.uniform(0.5, 2.0, shape) * np.where(np.random.standard_normal(shape) < 0, -1.0, 1.0)


K, T, J, F, Z, Q, O, R, N = 512, 1024, 256, 512, 1024, 128, 128, 512, 256


def setup_inputs():
    n = np.random.standard_normal
    idx = np.random.permutation(T)[:J]
    idx2 = np.random.permutation(Z)[:J]
    idx3 = np.random.permutation(J)[:O]
    idx4 = np.random.permutation(J)[:O]
    idx5 = np.random.permutation(J)[:O]
    idx6 = np.random.permutation(J)[:O]
    fk = mx_kscale(K)
    ff = mx_kscale(F)
    fr = mx_kscale(R)
    xtp = pack_weight(n((K, T)) / fk[:, None], "e2m1")
    xop = pack_weight(n((F, Z)) / ff[:, None], "e5m2")
    wp = pack_weight(n((K, Q)) * 1 / np.sqrt(K) * fk[:, None], "e5m2")
    w2p = pack_weight(n((K, Q)) * 1 / np.sqrt(K) * fk[:, None], "e4m3")
    w3p = pack_weight(n((F, Q)) * 1 / np.sqrt(F) * ff[:, None], "e4m3")
    w0p = pack_weight(n((F, Q)) * 1 / np.sqrt(F) * ff[:, None], "e4m3")
    wbp = pack_weight(n((R, N)) * 1 / np.sqrt(R) / fr[:, None], "e4m3")
    return {
        "xt_words": xtp[0],
        "xt_scales": xtp[1],
        "xo_words": xop[0],
        "xo_scales": xop[1],
        "w_words": wp[0],
        "w_scales": wp[1],
        "w2_words": w2p[0],
        "w2_scales": w2p[1],
        "w3_words": w3p[0],
        "w3_scales": w3p[1],
        "w0_words": w0p[0],
        "w0_scales": w0p[1],
        "sa": (np.random.uniform(0.5, 1.6, (Q, 1)) * fr[::4, None]).astype(np.float32),
        "sb": (sgn((Q, 1)) * fr[::4, None]).astype(np.float32),
        "sd": (np.random.uniform(0.5, 1.6, (Q, 1)) * fr[::4, None]).astype(np.float32),
        "se": (sgn((Q, 1)) * fr[::4, None]).astype(np.float32),
        "wb_words": wbp[0],
        "wb_scales": wbp[1],
        "offs": striped(idx),
        "offs2": striped(idx2),
        "offs3": striped(idx3),
        "offs4": striped(idx4),
        "offs5": striped(idx5),
        "offs6": striped(idx6),
    }


def reference(xt_words, xt_scales, xo_words, xo_scales, w_words, w_scales, w2_words, w2_scales, w3_words, w3_scales, w0_words, w0_scales, sa, sb, sd, se, wb_words, wb_scales, offs, offs2, offs3, offs4, offs5, offs6):
    idx = unstriped(offs)
    idx2 = unstriped(offs2)
    idx3 = unstriped(offs3)
    idx4 = unstriped(offs4)
    idx5 = unstriped(offs5)
    idx6 = unstriped(offs6)
    xtu = unpack_weight(xt_words, xt_scales, "e2m1")
    xou = unpack_weight(xo_words, xo_scales, "e5m2")
    wu = unpack_weight(w_words, w_scales, "e5m2")
    w2u = unpack_weight(w2_words, w2_scales, "e4m3")
    w3u = unpack_weight(w3_words, w3_scales, "e4m3")
    w0u = unpack_weight(w0_words, w0_scales, "e4m3")
    wbu = unpack_weight(wb_words, wb_scales, "e4m3")
    xtidxg = xtu[:, idx]
    a = wu.T @ xtidxg
    b = w2u.T @ xtidxg
    xoidx2g = xou[:, idx2]
    g = w3u.T @ xoidx2g
    d = w0u.T @ xoidx2g
    v0 = a[:, idx3] * f64(sa)
    v1 = g[:, idx4] * f64(sd)
    v2 = b[:, idx5] * f64(sb)
    v3 = d[:, idx6] * f64(se)
    hid = np.stack([v0, v1, v2, v3], axis=1).reshape(R, O)
    hidq = mxq(hid, 0, "e4m3")
    p = wbu.T @ hidq
    return p

@@ -1,0 +1,138 @@
+from contextlib import ExitStack
+
+import concourse.mybir as mybir
+
+F32 = mybir.dt.float32
+BF16 = mybir.dt.bfloat16
+I32 = mybir.dt.int32
+U32 = mybir.dt.uint32
+U16 = mybir.dt.uint16
+U8 = mybir.dt.uint8
+E4M3 = mybir.dt.float8_e4m3fn_x4
+E5M2 = mybir.dt.float8_e5m2_x4
+E2M1 = mybir.dt.float4_e2m1fn_x4
+COPY = mybir.ActivationFunctionType.Copy
+
+P = 128
+TABLE = 1024
+SLOTS = 256
+TOWER = 128
+PLACES = 128
+N_OUT = 256
+QUADS = 4
+FLOPS = 2 * 512 * (4 * TOWER * SLOTS + N_OUT * PLACES)
+
+
+def tile_list_fourtowers_kernel(tc, xt_words, xt_scales, xo_words, xo_scales, w_words, w_scales, w2_words, w2_scales,
+                                     w3_words, w3_scales, w0_words, w0_scales, sa, sb, sd, se, wb_words, wb_scales,
+                                     offs, offs2, offs3, offs4, offs5, offs6, out):
+    nc = tc.nc
+    with ExitStack() as ctx:
+        pool = ctx.enter_context(tc.tile_pool(name="sb", bufs=1))
+        psum = ctx.enter_context(tc.psum_pool(name="ps", bufs=1))
+
+        def sbuf(name, shape, dtype):
+            return pool.tile(shape, dtype, name=name, align_bytes=64)
+
+        def words_of(dram):
+            return dram[0].rearrange("p n t -> p (n t)").bitcast(I32)
+
+        lists = {}
+        for name, cols in (("offs", 16), ("offs2", 16), ("offs3", 8), ("offs4", 8), ("offs5", 8), ("offs6", 8)):
+            lists[name] = pool.tile([P, cols], U16, name="list_" + name)
+
+        xt_tab = sbuf("xt_tab", [P, TABLE], U16)
+        xt_plane = sbuf("xt_plane", [P, TABLE], U8)
+        xo_tab = sbuf("xo_tab", [P, TABLE], I32)
+        xo_plane = sbuf("xo_plane", [P, TABLE], U8)
+        tower_planes = sbuf("tower_planes", [P, QUADS, 4 * TOWER // 4], I32)
+        wb_planes = sbuf("wb_planes", [P, QUADS, N_OUT // 4], I32)
+        tower_words = [sbuf("tower_words%d" % i, [P, TOWER], I32) for i in range(4)]
+        wb_codes = sbuf("wb_codes", [P, N_OUT], I32)
+        factors = [sbuf("factor%d" % i, [P, 1], F32) for i in range(4)]
+
+        nc.vector.memset(xt_plane[:].bitcast(I32), 0)
+        nc.vector.memset(tower_planes[:, 0:3:2, :], 0)
+        nc.vector.memset(xo_plane[:].bitcast(I32), 0)
+        nc.vector.memset(wb_planes[:, 0:3:2, :], 0)
+
+        def load_table_plane(plane, scales):
+            for q in range(QUADS):
+                nc.sync.dma_start(plane[32 * q : 32 * q + 4, :].bitcast(I32), scales[0, 4 * q : 4 * q + 4, :].bitcast(I32))
+
+        def load_rows(dst, scales):
+            nc.sync.dma_start(dst, scales[0].bitcast(I32).rearrange("(q r) n -> r q n", r=4))
+
+        def spread(planes):
+            nc.vector.tensor_copy(planes[32:36, 0:3, :], planes[0:4, 1:4, :])
+            nc.vector.tensor_copy(planes[64:128, 0, :], planes[0:64, 2, :])
+
+        nc.gpsimd.dma_start(tower_words[0][:], words_of(w_words))
+        nc.gpsimd.dma_start(tower_words[1][:], words_of(w2_words))
+        for i, vec in enumerate((sa, sb, sd, se)):
+            nc.gpsimd.dma_start(factors[i][:], vec)
+
+        nc.sync.dma_start(lists["offs"][:], offs)
+        nc.sync.dma_start(xt_tab[:].bitcast(I32), xt_words[0].bitcast(I32))
+        nc.sync.dma_start(lists["offs2"][:], offs2)
+        nc.sync.dma_start(xo_tab[:], words_of(xo_words))
+        load_table_plane(xt_plane, xt_scales)
+        for i, scales in enumerate((w_scales, w2_scales, w3_scales, w0_scales)):
+            load_rows(tower_planes[0:4, :, 32 * i : 32 * (i + 1)], scales)
+        load_table_plane(xo_plane, xo_scales)
+        nc.sync.dma_start(lists["offs3"][:], offs3)
+        nc.sync.dma_start(tower_words[2][:], words_of(w3_words))
+        nc.sync.dma_start(tower_words[3][:], words_of(w0_words))
+        nc.sync.dma_start(lists["offs5"][:], offs5)
+        nc.sync.dma_start(lists["offs4"][:], offs4)
+        nc.sync.dma_start(lists["offs6"][:], offs6)
+        load_rows(wb_planes[0:4, :, :], wb_scales)
+        nc.sync.dma_start(wb_codes[:], words_of(wb_words))
+
+        xt_picked = sbuf("xt_picked", [P, SLOTS], U16)
+        xt_picked_plane = sbuf("xt_picked_plane", [P, SLOTS], U8)
+        xo_picked = sbuf("xo_picked", [P, SLOTS], U32)
+        xo_picked_plane = sbuf("xo_picked_plane", [P, SLOTS], U8)
+        nc.vector.tensor_copy(xt_picked[:], xt_tab[:].indirect(lists["offs"][:]))
+        nc.vector.tensor_copy(xt_picked_plane[:], xt_plane[:].indirect(lists["offs"][:]))
+        nc.vector.tensor_copy(xo_picked[:], xo_tab[:].bitcast(U32).indirect(lists["offs2"][:]))
+        spread(tower_planes)
+        nc.vector.tensor_copy(xo_picked_plane[:], xo_plane[:].indirect(lists["offs2"][:]))
+
+        hid = sbuf("hid", [P, 4 * PLACES], BF16)
+        plane_bytes = tower_planes[:, 0, :].bitcast(U8)
+        towers = (
+            (E5M2, xt_picked[:].bitcast(E2M1), xt_picked_plane, "offs3", 0),
+            (E4M3, xt_picked[:].bitcast(E2M1), xt_picked_plane, "offs5", 2),
+            (E4M3, xo_picked[:].bitcast(E5M2), xo_picked_plane, "offs4", 1),
+            (E4M3, xo_picked[:].bitcast(E5M2), xo_picked_plane, "offs6", 3),
+        )
+        for i, (fmt, moving, moving_plane, list_name, turn) in enumerate(towers):
+            acc = psum.tile([P, SLOTS], F32, name="acc%d" % i)
+            nc.tensor.matmul_mx(out=acc[:], lhsT=tower_words[i][:].bitcast(fmt), lhsT_scale=plane_bytes[:, TOWER * i : TOWER * (i + 1)],
+                                rhs=moving, rhs_scale=moving_plane[:], start=True, stop=True)
+            result = sbuf("result%d" % i, [P, SLOTS], F32)
+            if i == 0:
+                nc.scalar.copy(result[:], acc[:])
+            else:
+                nc.vector.tensor_copy(result[:], acc[:])
+            nc.scalar.activation(out=hid[:, turn : 4 * PLACES : 4], in_=result[:].indirect(lists[list_name][:]), func=COPY, scale=factors[i][:])
+
+        spread(wb_planes)
+        hid_codes = sbuf("hid_codes", [P, PLACES], U32)
+        hid_plane = sbuf("hid_plane", [P, PLACES], U8)
+        nc.vector.quantize_mx(out=hid_codes[:].bitcast(E4M3), scales=hid_plane[:], in_=hid[:])
+
+        wb_plane_bytes = wb_planes[:, 0, :].bitcast(U8)
+        for h in range(N_OUT // P):
+            cols = slice(P * h, P * (h + 1))
+            total = psum.tile([P, PLACES], F32, name="total%d" % h)
+            nc.tensor.matmul_mx(out=total[:], lhsT=wb_codes[:, cols].bitcast(E4M3), lhsT_scale=wb_plane_bytes[:, cols],
+                                rhs=hid_codes[:].bitcast(E4M3), rhs_scale=hid_plane[:], start=True, stop=True)
+            staged = sbuf("staged%d" % h, [P, PLACES], F32)
+            if h == 0:
+                nc.vector.tensor_copy(staged[:], total[:])
+                nc.sync.dma_start(out[cols, :], staged[:])
+            else:
+                nc.scalar.copy(staged[:], total[:])
+                nc.scalar.dma_start(out[cols, :], staged[:])

@@ -45,89 +45,99 @@ def tile_list_fourtowers_kernel(tc, xt_words, xt_scales, xo_words, xo_scales, w_
         xt_plane = sbuf("xt_plane", [P, TABLE], U8)
         xo_tab = sbuf("xo_tab", [P, TABLE], I32)
         xo_plane = sbuf("xo_plane", [P, TABLE], U8)
-        tower_planes = sbuf("tower_planes", [P, QUADS, 4 * TOWER // 4], I32)
-        wb_planes = sbuf("wb_planes", [P, QUADS, N_OUT // 4], I32)
+        tower_rows = sbuf("tower_rows", [4, QUADS, TOWER], I32)
+        tower_planes = sbuf("tower_planes", [P, 2, TOWER], I32)
+        wb_plane = sbuf("wb_plane", [P, N_OUT], U8)
         tower_words = [sbuf("tower_words%d" % i, [P, TOWER], I32) for i in range(4)]
         wb_codes = sbuf("wb_codes", [P, N_OUT], I32)
         factors = [sbuf("factor%d" % i, [P, 1], F32) for i in range(4)]
 
         nc.vector.memset(xt_plane[:].bitcast(I32), 0)
-        nc.vector.memset(tower_planes[:, 0:3:2, :], 0)
         nc.vector.memset(xo_plane[:].bitcast(I32), 0)
-        nc.vector.memset(wb_planes[:, 0:3:2, :], 0)
+        nc.vector.memset(tower_planes[0:64, :, :], 0)
+        nc.vector.memset(wb_plane[:].bitcast(I32), 0)
 
-        def load_table_plane(plane, scales):
-            for q in range(QUADS):
-                nc.sync.dma_start(plane[32 * q : 32 * q + 4, :].bitcast(I32), scales[0, 4 * q : 4 * q + 4, :].bitcast(I32))
+        def load_quadrant(queue, plane, scales, q):
+            queue.dma_start(plane[32 * q : 32 * q + 4, :].bitcast(I32), scales[0, 4 * q : 4 * q + 4, :].bitcast(I32))
 
-        def load_rows(dst, scales):
-            nc.sync.dma_start(dst, scales[0].bitcast(I32).rearrange("(q r) n -> r q n", r=4))
-
-        def spread(planes):
-            nc.vector.tensor_copy(planes[32:36, 0:3, :], planes[0:4, 1:4, :])
-            nc.vector.tensor_copy(planes[64:128, 0, :], planes[0:64, 2, :])
+        def load_rows(queue, i, scales):
+            queue.dma_start(tower_rows[:, :, 32 * i : 32 * (i + 1)], scales[0].bitcast(I32).rearrange("(q r) n -> r q n", r=4))
 
         nc.gpsimd.dma_start(tower_words[0][:], words_of(w_words))
+        load_quadrant(nc.gpsimd, xo_plane, xo_scales, 3)
         nc.gpsimd.dma_start(tower_words[1][:], words_of(w2_words))
-        for i, vec in enumerate((sa, sb, sd, se)):
-            nc.gpsimd.dma_start(factors[i][:], vec)
+        nc.gpsimd.dma_start(factors[1][:], sb)
+        nc.gpsimd.dma_start(factors[3][:], se)
 
+        load_rows(nc.scalar, 1, w2_scales)
         nc.sync.dma_start(lists["offs"][:], offs)
-        nc.sync.dma_start(xt_tab[:].bitcast(I32), xt_words[0].bitcast(I32))
+        load_rows(nc.scalar, 3, w0_scales)
+        load_rows(nc.sync, 0, w_scales)
+        nc.scalar.dma_start(xt_tab[:].bitcast(I32), xt_words[0].bitcast(I32))
+        load_rows(nc.sync, 2, w3_scales)
+        load_quadrant(nc.sync, xt_plane, xt_scales, 0)
+        nc.scalar.dma_start(xo_tab[:], words_of(xo_words))
+
+        load_quadrant(nc.sync, xt_plane, xt_scales, 1)
+        load_quadrant(nc.sync, xt_plane, xt_scales, 2)
+        load_quadrant(nc.scalar, xo_plane, xo_scales, 0)
+        load_quadrant(nc.sync, xt_plane, xt_scales, 3)
+        load_quadrant(nc.scalar, xo_plane, xo_scales, 1)
         nc.sync.dma_start(lists["offs2"][:], offs2)
-        nc.sync.dma_start(xo_tab[:], words_of(xo_words))
-        load_table_plane(xt_plane, xt_scales)
-        for i, scales in enumerate((w_scales, w2_scales, w3_scales, w0_scales)):
-            load_rows(tower_planes[0:4, :, 32 * i : 32 * (i + 1)], scales)
-        load_table_plane(xo_plane, xo_scales)
-        nc.sync.dma_start(lists["offs3"][:], offs3)
+        load_quadrant(nc.scalar, xo_plane, xo_scales, 2)
         nc.sync.dma_start(tower_words[2][:], words_of(w3_words))
+
+        nc.sync.dma_start(lists["offs3"][:], offs3)
+        nc.sync.dma_start(factors[0][:], sa)
         nc.sync.dma_start(tower_words[3][:], words_of(w0_words))
         nc.sync.dma_start(lists["offs5"][:], offs5)
         nc.sync.dma_start(lists["offs4"][:], offs4)
+        nc.sync.dma_start(factors[2][:], sd)
         nc.sync.dma_start(lists["offs6"][:], offs6)
-        load_rows(wb_planes[0:4, :, :], wb_scales)
         nc.sync.dma_start(wb_codes[:], words_of(wb_words))
+
+        for q in range(QUADS):
+            load_quadrant(nc.sync, wb_plane, wb_scales, q)
 
         xt_picked = sbuf("xt_picked", [P, SLOTS], U16)
         xt_picked_plane = sbuf("xt_picked_plane", [P, SLOTS], U8)
         xo_picked = sbuf("xo_picked", [P, SLOTS], U32)
         xo_picked_plane = sbuf("xo_picked_plane", [P, SLOTS], U8)
+        nc.vector.tensor_copy(tower_planes[0:4, :, :], tower_rows[:, 0:4:2, :])
+        nc.vector.tensor_copy(tower_planes[32:36, :, :], tower_rows[:, 1:4:2, :])
+        nc.vector.tensor_copy(tower_planes[64:128, 0, :], tower_planes[0:64, 1, :])
         nc.vector.tensor_copy(xt_picked[:], xt_tab[:].indirect(lists["offs"][:]))
         nc.vector.tensor_copy(xt_picked_plane[:], xt_plane[:].indirect(lists["offs"][:]))
         nc.vector.tensor_copy(xo_picked[:], xo_tab[:].bitcast(U32).indirect(lists["offs2"][:]))
-        spread(tower_planes)
         nc.vector.tensor_copy(xo_picked_plane[:], xo_plane[:].indirect(lists["offs2"][:]))
 
         hid = sbuf("hid", [P, 4 * PLACES], BF16)
         plane_bytes = tower_planes[:, 0, :].bitcast(U8)
         towers = (
-            (E5M2, xt_picked[:].bitcast(E2M1), xt_picked_plane, "offs3", 0),
-            (E4M3, xt_picked[:].bitcast(E2M1), xt_picked_plane, "offs5", 2),
-            (E4M3, xo_picked[:].bitcast(E5M2), xo_picked_plane, "offs4", 1),
-            (E4M3, xo_picked[:].bitcast(E5M2), xo_picked_plane, "offs6", 3),
+            (0, E5M2, xt_picked[:].bitcast(E2M1), xt_picked_plane, "offs3", 0),
+            (1, E4M3, xt_picked[:].bitcast(E2M1), xt_picked_plane, "offs5", 2),
+            (2, E4M3, xo_picked[:].bitcast(E5M2), xo_picked_plane, "offs4", 1),
+            (3, E4M3, xo_picked[:].bitcast(E5M2), xo_picked_plane, "offs6", 3),
         )
-        for i, (fmt, moving, moving_plane, list_name, turn) in enumerate(towers):
+        for i, fmt, moving, moving_plane, list_name, turn in towers:
             acc = psum.tile([P, SLOTS], F32, name="acc%d" % i)
             nc.tensor.matmul_mx(out=acc[:], lhsT=tower_words[i][:].bitcast(fmt), lhsT_scale=plane_bytes[:, TOWER * i : TOWER * (i + 1)],
                                 rhs=moving, rhs_scale=moving_plane[:], start=True, stop=True)
             result = sbuf("result%d" % i, [P, SLOTS], F32)
-            if i == 0:
+            if i < 2:
                 nc.scalar.copy(result[:], acc[:])
             else:
                 nc.vector.tensor_copy(result[:], acc[:])
             nc.scalar.activation(out=hid[:, turn : 4 * PLACES : 4], in_=result[:].indirect(lists[list_name][:]), func=COPY, scale=factors[i][:])
 
-        spread(wb_planes)
         hid_codes = sbuf("hid_codes", [P, PLACES], U32)
         hid_plane = sbuf("hid_plane", [P, PLACES], U8)
         nc.vector.quantize_mx(out=hid_codes[:].bitcast(E4M3), scales=hid_plane[:], in_=hid[:])
 
-        wb_plane_bytes = wb_planes[:, 0, :].bitcast(U8)
         for h in range(N_OUT // P):
             cols = slice(P * h, P * (h + 1))
             total = psum.tile([P, PLACES], F32, name="total%d" % h)
-            nc.tensor.matmul_mx(out=total[:], lhsT=wb_codes[:, cols].bitcast(E4M3), lhsT_scale=wb_plane_bytes[:, cols],
+            nc.tensor.matmul_mx(out=total[:], lhsT=wb_codes[:, cols].bitcast(E4M3), lhsT_scale=wb_plane[:, cols],
                                 rhs=hid_codes[:].bitcast(E4M3), rhs_scale=hid_plane[:], start=True, stop=True)
             staged = sbuf("staged%d" % h, [P, PLACES], F32)
             if h == 0:

@@ -128,11 +128,15 @@ def tile_list_fourtowers_kernel(tc, xt_words, xt_scales, xo_words, xo_scales, w_
                 nc.scalar.copy(result[:], acc[:])
             else:
                 nc.vector.tensor_copy(result[:], acc[:])
-            nc.scalar.activation(out=hid[:, turn : 4 * PLACES : 4], in_=result[:].indirect(lists[list_name][:]), func=COPY, scale=factors[i][:])
+            for half in range(2):
+                nc.scalar.activation(out=hid[:, 256 * half + turn : 256 * (half + 1) : 4], in_=result[:].indirect(lists[list_name][:, 4 * half : 4 * (half + 1)]),
+                                     func=COPY, scale=factors[i][:])
 
         hid_codes = sbuf("hid_codes", [P, PLACES], U32)
         hid_plane = sbuf("hid_plane", [P, PLACES], U8)
-        nc.vector.quantize_mx(out=hid_codes[:].bitcast(E4M3), scales=hid_plane[:], in_=hid[:])
+        for half in range(2):
+            nc.vector.quantize_mx(out=hid_codes[:, 64 * half : 64 * (half + 1)].bitcast(E4M3), scales=hid_plane[:, 64 * half : 64 * (half + 1)],
+                                  in_=hid[:, 256 * half : 256 * (half + 1)])
 
         for h in range(N_OUT // P):
             cols = slice(P * h, P * (h + 1))

from contextlib import ExitStack

import concourse.mybir as mybir

F32 = mybir.dt.float32
BF16 = mybir.dt.bfloat16
I32 = mybir.dt.int32
U32 = mybir.dt.uint32
U16 = mybir.dt.uint16
U8 = mybir.dt.uint8
E4M3 = mybir.dt.float8_e4m3fn_x4
E5M2 = mybir.dt.float8_e5m2_x4
E2M1 = mybir.dt.float4_e2m1fn_x4
COPY = mybir.ActivationFunctionType.Copy

P = 128
TABLE = 1024
SLOTS = 256
TOWER = 128
PLACES = 128
N_OUT = 256
QUADS = 4
FLOPS = 2 * 512 * (4 * TOWER * SLOTS + N_OUT * PLACES)


def tile_list_fourtowers_kernel(tc, xt_words, xt_scales, xo_words, xo_scales, w_words, w_scales, w2_words, w2_scales,
                                     w3_words, w3_scales, w0_words, w0_scales, sa, sb, sd, se, wb_words, wb_scales,
                                     offs, offs2, offs3, offs4, offs5, offs6, out):
    nc = tc.nc
    with ExitStack() as ctx:
        pool = ctx.enter_context(tc.tile_pool(name="sb", bufs=1))
        psum = ctx.enter_context(tc.psum_pool(name="ps", bufs=1))

        def sbuf(name, shape, dtype):
            return pool.tile(shape, dtype, name=name, align_bytes=64)

        def words_of(dram):
            return dram[0].rearrange("p n t -> p (n t)").bitcast(I32)

        lists = {}
        for name, cols in (("offs", 16), ("offs2", 16), ("offs3", 8), ("offs4", 8), ("offs5", 8), ("offs6", 8)):
            lists[name] = pool.tile([P, cols], U16, name="list_" + name)

        xt_tab = sbuf("xt_tab", [P, TABLE], U16)
        xt_plane = sbuf("xt_plane", [P, TABLE], U8)
        xo_tab = sbuf("xo_tab", [P, TABLE], I32)
        xo_plane = sbuf("xo_plane", [P, TABLE], U8)
        tower_rows = sbuf("tower_rows", [4, QUADS, TOWER], I32)
        tower_planes = sbuf("tower_planes", [P, 2, TOWER], I32)
        wb_plane = sbuf("wb_plane", [P, N_OUT], U8)
        tower_words = [sbuf("tower_words%d" % i, [P, TOWER], I32) for i in range(4)]
        wb_codes = sbuf("wb_codes", [P, N_OUT], I32)
        factors = [sbuf("factor%d" % i, [P, 1], F32) for i in range(4)]

        nc.vector.memset(xt_plane[:].bitcast(I32), 0)
        nc.vector.memset(xo_plane[:].bitcast(I32), 0)
        nc.vector.memset(tower_planes[0:64, :, :], 0)
        nc.vector.memset(wb_plane[:].bitcast(I32), 0)

        def load_quadrant(queue, plane, scales, q):
            queue.dma_start(plane[32 * q : 32 * q + 4, :].bitcast(I32), scales[0, 4 * q : 4 * q + 4, :].bitcast(I32))

        def load_rows(queue, i, scales):
            queue.dma_start(tower_rows[:, :, 32 * i : 32 * (i + 1)], scales[0].bitcast(I32).rearrange("(q r) n -> r q n", r=4))

        nc.gpsimd.dma_start(tower_words[0][:], words_of(w_words))
        load_quadrant(nc.gpsimd, xo_plane, xo_scales, 3)
        nc.gpsimd.dma_start(tower_words[1][:], words_of(w2_words))
        nc.gpsimd.dma_start(factors[1][:], sb)
        nc.gpsimd.dma_start(factors[3][:], se)

        load_rows(nc.scalar, 1, w2_scales)
        nc.sync.dma_start(lists["offs"][:], offs)
        load_rows(nc.scalar, 3, w0_scales)
        load_rows(nc.sync, 0, w_scales)
        nc.scalar.dma_start(xt_tab[:].bitcast(I32), xt_words[0].bitcast(I32))
        load_rows(nc.sync, 2, w3_scales)
        load_quadrant(nc.sync, xt_plane, xt_scales, 0)
        nc.scalar.dma_start(xo_tab[:], words_of(xo_words))

        load_quadrant(nc.sync, xt_plane, xt_scales, 1)
        load_quadrant(nc.sync, xt_plane, xt_scales, 2)
        load_quadrant(nc.scalar, xo_plane, xo_scales, 0)
        load_quadrant(nc.sync, xt_plane, xt_scales, 3)
        load_quadrant(nc.scalar, xo_plane, xo_scales, 1)
        nc.sync.dma_start(lists["offs2"][:], offs2)
        load_quadrant(nc.scalar, xo_plane, xo_scales, 2)
        nc.sync.dma_start(tower_words[2][:], words_of(w3_words))

        nc.sync.dma_start(lists["offs3"][:], offs3)
        nc.sync.dma_start(factors[0][:], sa)
        nc.sync.dma_start(tower_words[3][:], words_of(w0_words))
        nc.sync.dma_start(lists["offs5"][:], offs5)
        nc.sync.dma_start(lists["offs4"][:], offs4)
        nc.sync.dma_start(factors[2][:], sd)
        nc.sync.dma_start(lists["offs6"][:], offs6)
        nc.sync.dma_start(wb_codes[:], words_of(wb_words))

        for q in range(QUADS):
            load_quadrant(nc.sync, wb_plane, wb_scales, q)

        xt_picked = sbuf("xt_picked", [P, SLOTS], U16)
        xt_picked_plane = sbuf("xt_picked_plane", [P, SLOTS], U8)
        xo_picked = sbuf("xo_picked", [P, SLOTS], U32)
        xo_picked_plane = sbuf("xo_picked_plane", [P, SLOTS], U8)
        nc.vector.tensor_copy(tower_planes[0:4, :, :], tower_rows[:, 0:4:2, :])
        nc.vector.tensor_copy(tower_planes[32:36, :, :], tower_rows[:, 1:4:2, :])
        nc.vector.tensor_copy(tower_planes[64:128, 0, :], tower_planes[0:64, 1, :])
        nc.vector.tensor_copy(xt_picked[:], xt_tab[:].indirect(lists["offs"][:]))
        nc.vector.tensor_copy(xt_picked_plane[:], xt_plane[:].indirect(lists["offs"][:]))
        nc.vector.tensor_copy(xo_picked[:], xo_tab[:].bitcast(U32).indirect(lists["offs2"][:]))
        nc.vector.tensor_copy(xo_picked_plane[:], xo_plane[:].indirect(lists["offs2"][:]))

        hid = sbuf("hid", [P, 4 * PLACES], BF16)
        plane_bytes = tower_planes[:, 0, :].bitcast(U8)
        towers = (
            (0, E5M2, xt_picked[:].bitcast(E2M1), xt_picked_plane, "offs3", 0),
            (1, E4M3, xt_picked[:].bitcast(E2M1), xt_picked_plane, "offs5", 2),
            (2, E4M3, xo_picked[:].bitcast(E5M2), xo_picked_plane, "offs4", 1),
            (3, E4M3, xo_picked[:].bitcast(E5M2), xo_picked_plane, "offs6", 3),
        )
        for i, fmt, moving, moving_plane, list_name, turn in towers:
            acc = psum.tile([P, SLOTS], F32, name="acc%d" % i)
            nc.tensor.matmul_mx(out=acc[:], lhsT=tower_words[i][:].bitcast(fmt), lhsT_scale=plane_bytes[:, TOWER * i : TOWER * (i + 1)],
                                rhs=moving, rhs_scale=moving_plane[:], start=True, stop=True)
            result = sbuf("result%d" % i, [P, SLOTS], F32)
            if i < 2:
                nc.scalar.copy(result[:], acc[:])
            else:
                nc.vector.tensor_copy(result[:], acc[:])
            for half in range(2):
                nc.scalar.activation(out=hid[:, 256 * half + turn : 256 * (half + 1) : 4], in_=result[:].indirect(lists[list_name][:, 4 * half : 4 * (half + 1)]),
                                     func=COPY, scale=factors[i][:])

        hid_codes = sbuf("hid_codes", [P, PLACES], U32)
        hid_plane = sbuf("hid_plane", [P, PLACES], U8)
        for half in range(2):
            nc.vector.quantize_mx(out=hid_codes[:, 64 * half : 64 * (half + 1)].bitcast(E4M3), scales=hid_plane[:, 64 * half : 64 * (half + 1)],
                                  in_=hid[:, 256 * half : 256 * (half + 1)])

        for h in range(N_OUT // P):
            cols = slice(P * h, P * (h + 1))
            total = psum.tile([P, PLACES], F32, name="total%d" % h)
            nc.tensor.matmul_mx(out=total[:], lhsT=wb_codes[:, cols].bitcast(E4M3), lhsT_scale=wb_plane[:, cols],
                                rhs=hid_codes[:].bitcast(E4M3), rhs_scale=hid_plane[:], start=True, stop=True)
            staged = sbuf("staged%d" % h, [P, PLACES], F32)
            if h == 0:
                nc.vector.tensor_copy(staged[:], total[:])
                nc.sync.dma_start(out[cols, :], staged[:])
            else:
                nc.scalar.copy(staged[:], total[:])
                nc.scalar.dma_start(out[cols, :], staged[:])
